import numpy as np, ml_dtypes
CORES = [24,48,72,152,176,200]
N = 6
import mx_ref
NC = 192
BF = ml_dtypes.bfloat16
def cut(t, i, w=512):
    return t[:, w * i:w * i + w]
def tile(rs):
    return np.stack(rs, axis=2).reshape(128, -1).astype(BF)
def onehot(t, r):
    own, p, b = t[:, :NC], t[:, NC:2 * NC], t[:, 2 * NC:]
    return tile([((own == r) & (p == np.arange(128)[:, None]) & (b == f)).astype(np.float32) for f in range(4)])
def setup_inputs(rng):
    def f(*shape):
        return mx_ref.flush((rng.standard_normal(shape, dtype=np.float32) * np.exp2(rng.integers(-2, 3, shape[:-1] + (1,)))).astype(BF))
    t = np.concatenate([rng.integers(0, N, (N, 1, NC)), rng.integers(0, 128, (N, 1, NC)), rng.integers(0, 4, (N, 1, NC))], axis=2)
    return {"tg": np.broadcast_to(t, (N, 128, 3 * NC)).astype(BF).copy(), "tab": f(N, 128, 4 * 512), "w": f(N, 128, 512)}
def setup_inputs_blocks(rng):
    d = setup_inputs(rng)
    for k in ("tab", "w"): d[k] = mx_ref.spread(d[k], rng, 4)
    return d
def setup_inputs_wide(rng):
    d = setup_inputs(rng)
    for k in ("tab", "w"): d[k] = mx_ref.flush((d[k].astype(np.float32) * np.exp2(rng.integers(-6, 7, (N, 1, 1))).astype(np.float32)).astype(BF))
    return d
def setup_inputs_hot(rng):
    d = setup_inputs(rng); t = d["tg"].astype(np.float32); t[:, :, :NC] = rng.integers(0, N); t[:, :, NC:2 * NC] = np.broadcast_to(rng.integers(0, 4, (N, 1, NC)), (N, 128, NC))
    d["tg"] = t.astype(BF)
    return d
def reference(tg, tab, w):
    y = np.zeros((N, 128, NC), np.float32)
    for j in range(N):
        qw = mx_ref.quantize(w[j])
        for r in range(N):
            o = mx_ref.quantize(onehot(tg[j].astype(np.float32), r))
            e = mx_ref.quantize(tile([mx_ref.matmul(mx_ref.quantize(cut(tab[r], f)), o) for f in range(4)]))
            p = mx_ref.matmul(qw, e)
            y[j] = p if r == 0 else y[j] + p
    return {"y": y}

@@ -1,0 +1,330 @@
+import math
+from concourse.bass import DstId, RemoteDMATransfer
+from concourse.mybir import AluOpType, ActivationFunctionType, dt
+
+N = 6
+NC = 192
+G = 32
+K = NC // G
+SL = 8
+SIM = 256
+
+SCRATCH = {
+    "idl": ("sbuf", [128, 3 * SL], "bfloat16"),
+    "idf": ("sbuf", [128, 3 * SL], "bfloat16"),
+    "idu": ("sbuf", [128, SL], "bfloat16"),
+    "x": ("sbuf", [128, SL], "bfloat16"),
+    "xin": ("sbuf", [128, N * SL], "bfloat16"),
+    "xrel": ("sbuf", [128, SL], "bfloat16"),
+    "ip": ("sbuf", [128, 1], "float32"),
+    "ij": ("sbuf", [128, 4], "float32"),
+    "pw": ("sbuf", [128, 4], "bfloat16"),
+    "key": ("sbuf", [128, 4], "float32"),
+    "hold": ("sbuf", [128, NC], "bfloat16"),
+    "seed": ("sbuf", [128, N * NC], "bfloat16"),
+    "spr": ("sbuf", [128, N * NC], "bfloat16"),
+    "xt": ("sbuf", [128, N * NC], "bfloat16"),
+    "o": ("sbuf", [128, N * 4 * NC], "bfloat16"),
+    "qo": ("sbuf", [128, N * NC], "float8_e4m3fn_x4"),
+    "so": ("sbuf", [128, N * NC], "uint8"),
+    "tb": ("sbuf", [128, 4 * 512], "bfloat16"),
+    "qt": ("sbuf", [128, 512], "float8_e4m3fn_x4"),
+    "st": ("sbuf", [128, 512], "uint8"),
+    "wb": ("sbuf", [128, 512], "bfloat16"),
+    "qw": ("sbuf", [128, 128], "float8_e4m3fn_x4"),
+    "sw": ("sbuf", [128, 128], "uint8"),
+    "e": ("sbuf", [128, N * 4 * NC], "bfloat16"),
+    "qe": ("sbuf", [128, N * NC], "float8_e4m3fn_x4"),
+    "se": ("sbuf", [128, N * NC], "uint8"),
+    "lc": ("sbuf", [128, N * NC], "float8_e4m3fn_x4"),
+    "ls": ("sbuf", [128, N * NC], "uint8"),
+    "rc": ("sbuf", [128, 2 * NC], "float8_e4m3fn_x4"),
+    "rs": ("sbuf", [128, 2 * NC], "uint8"),
+    "ysb": ("sbuf", [128, NC], "float32"),
+    "z": ("psum", [128, 8 * 512], "float32"),
+}
+SEMAPHORES = (["ldo", "ldp", "ldb", "ldt0", "ldt1", "ldw", "iop", "ioj", "exk", "exo", "exb", "ms", "mh", "mz", "kk", "pa", "uu", "xx",
+               "rid", "sent", "qws", "yy", "yv", "yst"]
+              + ["qt%d" % f for f in range(4)]
+              + ["rc%d" % i for i in range(2)] + ["rs%d" % i for i in range(2)]
+              + [s + str(t) for s in ("id", "cp", "sc", "tr", "cm", "qo", "ev", "qe", "ar") for t in range(N)]
+              + ["z%d_%d" % (t, f) for t in range(N) for f in range(4)])
+
+
+def engines(mask):
+    return [i for i in range(16) if mask >> i & 1]
+
+
+def bits(es):
+    return sum(1 << i for i in es)
+
+
+def plan(cores, topo):
+    out = []
+    flip = [0, 0]
+    for r, c in enumerate(cores):
+        near = [j for j in range(N) if j != r and topo.may_write(c, cores[j])]
+        far = [j for j in range(N) if j != r and j not in near]
+        helpers = [h for h in range(SIM)
+                   if h != c and topo.chip(h) == topo.chip(c) and topo.host(h) == topo.host(c)
+                   and all(topo.may_write(h, cores[j]) for j in far)]
+        same = [h for h in helpers if topo.die(h) == topo.die(c)]
+        other = [h for h in helpers if topo.die(h) != topo.die(c)]
+        if len(far) > 2:
+            s = flip[0] % 2
+            flip[0] += 1
+            far = far[s:] + far[:s]
+            relays = [(same[0], far[0::2]), (other[0], far[1::2])]
+        else:
+            s = flip[1] in (1, 2)
+            flip[1] += 1
+            relays = [((other if s else same)[0], far)]
+        out.append({"near": near, "far": far, "relays": relays})
+    return out
+
+
+def ids_calls(topo, cores, order, r):
+    c, p = cores[r], order[r]
+    low = engines(topo.mask(c, cores[p["near"][0]]))
+    high = [e for e in engines(topo.mask(c, p["relays"][0][0])) if e not in low]
+    if len(p["relays"]) > 1:
+        n = len(high) // 2
+        return [[(h, high[n * i:n * i + n]) for i, (h, _) in enumerate(p["relays"])] + [(cores[j], low[:n]) for j in p["near"]]]
+    return [[(p["relays"][0][0], low[:4])],
+            [(cores[j], low[2 + 2 * i:4 + 2 * i]) for i, j in enumerate(p["near"])]]
+
+
+def ids_count(topo, cores, order, r, to):
+    return [len(es) for call in ids_calls(topo, cores, order, r) for d, es in call if d == to][0]
+
+
+def near_engines(topo, cores, order, r, j):
+    es = engines(topo.mask(cores[r], cores[j]))
+    i = order[r]["near"].index(j)
+    if i == 0:
+        return es
+    n = len(es) // 2
+    return es[n * (i - 1):n * i]
+
+
+def relay_count(topo, core, relay):
+    return engines(topo.mask(core, relay))
+
+
+def dst(topo, to, frm):
+    rid, pnc = topo.addr(to, frm)
+    return DstId(rid=rid, pnc=pnc)
+
+
+def send(g, T, topo, core, parts):
+    g.remote_dma_fused([RemoteDMATransfer(dst_ids=[dst(topo, to, core)], dma_engine_mask=bits(es), remote_sem=sem, src=in_, dst=out)
+                        for to, out, in_, sem, es in parts], local_sem=T.sem.sent)
+    return sum(len(p[4]) for p in parts)
+
+
+def cut(buf, t, w=NC):
+    return buf[:, w * t:w * t + w]
+
+
+def codes(buf, t):
+    return cut(buf, t).bitcast(dt.uint8)
+
+
+def relay_program(g, core, T, topo, r, far, order):
+    cores, S = T.cores, T.sem
+    es = engines(topo.mask(core, cores[far[0]]))
+    n = len(es) // len(far)
+    ar, m = S["ar%d" % r], len(relay_count(topo, cores[r], core))
+    g.wait_ge(S.rid, ids_count(topo, cores, order, r, core))
+    sent = send(g, T, topo, core, [(cores[j], T.xin[:, SL * r:SL * r + K], T.xrel[:, 0:K], S["id%d" % r], es[n * i:n * i + n])
+                                   for i, j in enumerate(far)])
+    for i, j in enumerate(far):
+        g.wait_ge(S["rc%d" % i], m)
+        sent += send(g, T, topo, core, [(cores[j], codes(T.lc, r), codes(T.rc, i), ar, es)])
+        g.wait_ge(S["rs%d" % i], m)
+        sent += send(g, T, topo, core, [(cores[j], cut(T.ls, r), cut(T.rs, i), ar, es)])
+    g.wait_ge(S.sent, sent)
+
+
+def rank_program(g, core, T, topo):
+    rank = T.rank_of(core)
+    cores = T.cores
+    if rank is None and not any(topo.chip(core) == topo.chip(c) and topo.host(core) == topo.host(c) for c in cores):
+        return
+    order = plan(cores, topo)
+    if rank is None:
+        for r in range(N):
+            for h, far in order[r]["relays"]:
+                if h == core:
+                    relay_program(g, core, T, topo, r, far, order)
+        return
+    A, F = AluOpType, ActivationFunctionType
+    S = T.sem
+    v, ac, te, sy = g.vector, g.scalar, g.tensor, g.sync
+    near, far, relays = order[rank]["near"], order[rank]["far"], order[rank]["relays"]
+    work = [rank] + near + far
+
+    sy.dma_start(T.idl[:, 0:K], T.tg[0:4, 0:NC]).then_inc(S.ldo, 16)
+    ac.dma_start(T.idl[:, 2 * SL:2 * SL + K], T.tg[0:4, 2 * NC:3 * NC]).then_inc(S.ldb, 16)
+    sy.dma_start(T.idl[:, SL:SL + K], T.tg[0:4, NC:2 * NC]).then_inc(S.ldp, 16)
+    sy.dma_start(T.tb[:, 0:1024], T.tab[:, 0:1024]).then_inc(S.ldt0, 16)
+    sy.dma_start(T.tb[:, 1024:2048], T.tab[:, 1024:2048]).then_inc(S.ldt1, 16)
+    sy.dma_start(T.wb[:], T.w[:]).then_inc(S.ldw, 16)
+
+    g.iota(T.ij[:], [[1, 4]], 4 * rank, 0, allow_small_or_imprecise_dtypes=True).then_inc(S.ioj, 1)
+    g.iota(T.ip[:], [[1, 1]], 128, 1, allow_small_or_imprecise_dtypes=True).then_inc(S.iop, 1)
+    v.memset(T.hold[:], 1.0).then_inc(S.mh, 1)
+    v.memset(T.seed[:], 0.0).then_inc(S.ms, 1)
+    v.wait_ge(S.mh, 1)
+    v.memset(T.hold[:, 0:NC:G], 0.0).then_inc(S.mz, 1)
+
+    ln2 = math.log(2.0)
+    ac.wait_ge(S.ioj, 1)
+    ac.activation(T.pw[:], T.ij[:], F.Exp, scale=ln2).then_inc(S.exk, 1)
+    ac.wait_ge(S.ldo, 16)
+    ac.activation(T.idf[:, 0:K], T.idl[:, 0:K], F.Exp, scale=4 * ln2).then_inc(S.exo, 1)
+    ac.wait_ge(S.ldb, 16)
+    ac.activation(T.idf[:, 2 * SL:2 * SL + K], T.idl[:, 2 * SL:2 * SL + K], F.Exp, scale=ln2).then_inc(S.exb, 1)
+
+    v.wait_ge(S.ldp, 16)
+    v.tensor_scalar(T.idf[:, SL:SL + K], T.idl[:, SL:SL + K], 128.0, None, A.add).then_inc(S.pa, 1)
+    v.wait_ge(S.pa, 1)
+    v.wait_ge(S.exo, 1)
+    v.tensor_tensor(T.idu[:, 0:K], T.idf[:, SL:SL + K], T.idf[:, 0:K], A.mult).then_inc(S.uu, 1)
+    v.wait_ge(S.uu, 1)
+    v.wait_ge(S.exb, 1)
+    v.tensor_tensor(T.x[:, 0:K], T.idu[:, 0:K], T.idf[:, 2 * SL:2 * SL + K], A.mult).then_inc(S.xx, 1)
+
+    sent = 0
+    g.wait_ge(S.xx, 1)
+    for call in ids_calls(topo, cores, order, rank):
+        parts = []
+        for d, es in call:
+            if T.rank_of(d) is None:
+                parts.append((d, T.xrel[:, 0:K], T.x[:, 0:K], S.rid, es))
+            else:
+                parts.append((d, T.xin[:, SL * rank:SL * rank + K], T.x[:, 0:K], S["id%d" % rank], es))
+        sent += send(g, T, topo, core, parts)
+
+    def id_count(r):
+        if rank in order[r]["near"]:
+            return ids_count(topo, cores, order, r, core)
+        for h, fr in order[r]["relays"]:
+            if rank in fr:
+                return len(engines(topo.mask(h, core))) // len(fr)
+
+    def spread(ts):
+        for t in ts:
+            j = work[t]
+            if j == rank:
+                v.wait_ge(S.xx, 1)
+                src = T.x[:, 0:K]
+            else:
+                v.wait_ge(S["id%d" % j], id_count(j))
+                src = T.xin[:, SL * j:SL * j + K]
+            v.tensor_copy(T.seed[:, NC * t:NC * t + NC:G], src).then_inc(S["cp%d" % t], 1)
+        for t in ts:
+            v.wait_ge(S["cp%d" % t], 1)
+            v.tensor_tensor_scan(cut(T.spr, t), T.hold[:], cut(T.seed, t), 0.0, A.mult, A.add).then_inc(S["sc%d" % t], 1)
+        for t in ts:
+            v.wait_ge(S["sc%d" % t], 1)
+            v.transpose(cut(T.xt, t), cut(T.spr, t)).then_inc(S["tr%d" % t], 1)
+
+    def match(t):
+        v.wait_ge(S["tr%d" % t], 1)
+        for b in range(4):
+            v.tensor_scalar(T.o[:, 4 * NC * t + b:4 * NC * (t + 1):4], cut(T.xt, t), T.key[:, b:b + 1], None,
+                            A.is_equal).then_inc(S["cm%d" % t], 1)
+        v.wait_ge(S["cm%d" % t], 4)
+        v.quantize_mx(cut(T.qo, t), cut(T.so, t), cut(T.o, t, 4 * NC)).then_inc(S["qo%d" % t], 1)
+
+    def pack(t):
+        v.wait_ge(S["ev%d" % t], 4)
+        v.quantize_mx(cut(T.qe, t), cut(T.se, t), cut(T.e, t, 4 * NC)).then_inc(S["qe%d" % t], 1)
+
+    v.wait_ge(S.ms, 1)
+    v.wait_ge(S.mz, 1)
+    spread([0])
+    v.wait_ge(S.exk, 1)
+    v.wait_ge(S.iop, 1)
+    v.tensor_scalar(T.key[:], T.pw[:], T.ip[:, 0:1], None, A.mult).then_inc(S.kk, 1)
+    v.wait_ge(S.kk, 1)
+    match(0)
+    for f in range(4):
+        if f % 2 == 0:
+            v.wait_ge(S["ldt%d" % (f // 2)], 16)
+        v.quantize_mx(cut(T.qt, f, 128), cut(T.st, f, 128), cut(T.tb, f, 512)).then_inc(S["qt%d" % f], 1)
+    v.wait_ge(S.ldw, 16)
+    v.quantize_mx(T.qw[:], T.sw[:], T.wb[:]).then_inc(S.qws, 1)
+    pack(0)
+    if len(near) == 3:
+        steps = [(spread, [1, 2]), (match, 1), (match, 2), (spread, [3]), (pack, 1), (match, 3), (pack, 2), (pack, 3),
+                 (spread, [4, 5]), (match, 4), (match, 5), (pack, 4), (pack, 5)]
+    else:
+        steps = [(spread, [1]), (match, 1), (pack, 1), (spread, [2, 3]), (match, 2), (match, 3), (spread, [4, 5]),
+                 (pack, 2), (match, 4), (pack, 3), (match, 5), (pack, 4), (pack, 5)]
+    for step, t in steps:
+        step(t)
+
+    for t in range(N):
+        te.wait_ge(S["qo%d" % t], 1)
+        if t >= 2:
+            te.wait_ge(S["ev%d" % (t - 2)], 4)
+        for f in range(4):
+            if t == 0:
+                te.wait_ge(S["qt%d" % f], 1)
+            bank = 512 * (4 * (t % 2) + f)
+            te.matmul_mx(T.z[:, bank:bank + NC], cut(T.qt, f, 128), cut(T.st, f, 128), cut(T.qo, t), cut(T.so, t), True, True
+                         ).then_inc(S["z%d_%d" % (t, f)], 1)
+
+    for t in range(N):
+        for f in range(4):
+            bank = 512 * (4 * (t % 2) + f)
+            ac.wait_ge(S["z%d_%d" % (t, f)], 1)
+            ac.activation(T.e[:, 4 * NC * t + f:4 * NC * (t + 1):4], T.z[:, bank:bank + NC], F.Copy).then_inc(S["ev%d" % t], 1)
+
+    groups = [[1]] + ([[2, 3]] if len(near) == 3 else []) + [[t] for t in range(1 + len(near), N)]
+    for ts in groups:
+        for t in ts:
+            g.wait_ge(S["qe%d" % t], 1)
+        pc, ps = [], []
+        for t in ts:
+            j = work[t]
+            if j in near:
+                es, ar = near_engines(topo, cores, order, rank, j), S["ar%d" % rank]
+                pc.append((cores[j], codes(T.lc, rank), codes(T.qe, t), ar, es))
+                ps.append((cores[j], cut(T.ls, rank), cut(T.se, t), ar, es))
+            else:
+                h, fr = [(h, fr) for h, fr in relays if j in fr][0]
+                i, es = fr.index(j), relay_count(topo, core, h)
+                pc.append((h, codes(T.rc, i), codes(T.qe, t), S["rc%d" % i], es))
+                ps.append((h, cut(T.rs, i), cut(T.se, t), S["rs%d" % i], es))
+        sent += send(g, T, topo, core, pc)
+        sent += send(g, T, topo, core, ps)
+
+    def tile_count(r):
+        if rank in order[r]["near"]:
+            return 2 * len(near_engines(topo, cores, order, r, rank))
+        for h, fr in order[r]["relays"]:
+            if rank in fr:
+                return 2 * len(engines(topo.mask(h, core)))
+
+    te.wait_ge(S.qws, 1)
+    te.wait_ge(S["ev4"], 4)
+    for t in range(N):
+        j = work[t]
+        if t == 0:
+            te.wait_ge(S.qe0, 1)
+            c, s = cut(T.qe, 0), cut(T.se, 0)
+        else:
+            te.wait_ge(S["ar%d" % j], tile_count(j))
+            c, s = cut(T.lc, j), cut(T.ls, j)
+        mm = te.matmul_mx(T.z[:, 0:NC], T.qw[:], T.sw[:], c, s, t == 0, t == N - 1)
+    mm.then_inc(S.yy, 1)
+    v.wait_ge(S.yy, 1)
+    for k in range(K):
+        v.tensor_copy(T.ysb[:, k:NC:K], T.z[:, G * k:G * k + G]).then_inc(S.yv, 1)
+    sy.wait_ge(S.yv, K)
+    sy.dma_start(T.y[:], T.ysb[:]).then_inc(S.yst, 16)
+    sy.wait_ge(S.yst, 16)
+    g.wait_ge(S.sent, sent)

@@ -8,6 +8,7 @@ G = 32
 K = NC // G
 SL = 8
 SIM = 256
+CODES, SCALES = 0, 1
 
 SCRATCH = {
     "idl": ("sbuf", [128, 3 * SL], "bfloat16"),
@@ -19,7 +20,7 @@ SCRATCH = {
     "ip": ("sbuf", [128, 1], "float32"),
     "ij": ("sbuf", [128, 4], "float32"),
     "pw": ("sbuf", [128, 4], "bfloat16"),
-    "key": ("sbuf", [128, 4], "float32"),
+    "key": ("sbuf", [128, 4], "bfloat16"),
     "hold": ("sbuf", [128, NC], "bfloat16"),
     "seed": ("sbuf", [128, N * NC], "bfloat16"),
     "spr": ("sbuf", [128, N * NC], "bfloat16"),
@@ -38,16 +39,15 @@ SCRATCH = {
     "se": ("sbuf", [128, N * NC], "uint8"),
     "lc": ("sbuf", [128, N * NC], "float8_e4m3fn_x4"),
     "ls": ("sbuf", [128, N * NC], "uint8"),
-    "rc": ("sbuf", [128, 2 * NC], "float8_e4m3fn_x4"),
-    "rs": ("sbuf", [128, 2 * NC], "uint8"),
+    "rc": ("sbuf", [128, N * NC], "float8_e4m3fn_x4"),
+    "rs": ("sbuf", [128, N * NC], "uint8"),
     "ysb": ("sbuf", [128, NC], "float32"),
     "z": ("psum", [128, 8 * 512], "float32"),
 }
 SEMAPHORES = (["ldo", "ldp", "ldb", "ldt0", "ldt1", "ldw", "iop", "ioj", "exk", "exo", "exb", "ms", "mh", "mz", "kk", "pa", "uu", "xx",
                "rid", "sent", "qws", "yy", "yv", "yst"]
               + ["qt%d" % f for f in range(4)]
-              + ["rc%d" % i for i in range(2)] + ["rs%d" % i for i in range(2)]
-              + [s + str(t) for s in ("id", "cp", "sc", "tr", "cm", "qo", "ev", "qe", "ar") for t in range(N)]
+              + [s + str(t) for s in ("id", "cp", "sc", "tr", "cm", "qo", "ev", "qe", "ar", "rc", "rs") for t in range(N)]
               + ["z%d_%d" % (t, f) for t in range(N) for f in range(4)])
 
 
@@ -59,56 +59,66 @@ def bits(es):
     return sum(1 << i for i in es)
 
 
+def share(es, i, n):
+    k = len(es) // n
+    return es[k * i:k * i + k]
+
+
 def plan(cores, topo):
     out = []
-    flip = [0, 0]
-    for r, c in enumerate(cores):
-        near = [j for j in range(N) if j != r and topo.may_write(c, cores[j])]
-        far = [j for j in range(N) if j != r and j not in near]
+    seen = {}
+    for c in cores:
+        near = [j for j in range(N) if cores[j] != c and topo.may_write(c, cores[j])]
+        far = [j for j in range(N) if cores[j] != c and j not in near]
         helpers = [h for h in range(SIM)
                    if h != c and topo.chip(h) == topo.chip(c) and topo.host(h) == topo.host(c)
                    and all(topo.may_write(h, cores[j]) for j in far)]
         same = [h for h in helpers if topo.die(h) == topo.die(c)]
         other = [h for h in helpers if topo.die(h) != topo.die(c)]
-        if len(far) > 2:
-            s = flip[0] % 2
-            flip[0] += 1
-            far = far[s:] + far[:s]
-            relays = [(same[0], far[0::2]), (other[0], far[1::2])]
-        else:
-            s = flip[1] in (1, 2)
-            flip[1] += 1
-            relays = [((other if s else same)[0], far)]
-        out.append({"near": near, "far": far, "relays": relays})
+        relays = [h for two in zip(same, other) for h in two][:len(far)]
+        k = seen.get(len(far), 0)
+        seen[len(far)] = k + 1
+        s = k * len(far) // 4 % 2
+        flip = k % 2 if len(far) == 2 else 0
+        far = far[s:] + far[:s]
+        n = max(1, len(far) // 2)
+        out.append({"near": near, "far": far, "relays": relays, "ids": [(h, far[i::n]) for i, h in enumerate(relays[:n])],
+                    "carry": {j: (relays[i ^ flip], relays[i ^ flip ^ 1]) for i, j in enumerate(far)}})
     return out
 
 
+def low_high(topo, cores, order, r):
+    low = engines(topo.mask(cores[r], cores[order[r]["near"][0]]))
+    return low, [e for e in engines(topo.mask(cores[r], order[r]["relays"][0])) if e not in low]
+
+
 def ids_calls(topo, cores, order, r):
-    c, p = cores[r], order[r]
-    low = engines(topo.mask(c, cores[p["near"][0]]))
-    high = [e for e in engines(topo.mask(c, p["relays"][0][0])) if e not in low]
-    if len(p["relays"]) > 1:
-        n = len(high) // 2
-        return [[(h, high[n * i:n * i + n]) for i, (h, _) in enumerate(p["relays"])] + [(cores[j], low[:n]) for j in p["near"]]]
-    return [[(p["relays"][0][0], low[:4])],
-            [(cores[j], low[2 + 2 * i:4 + 2 * i]) for i, j in enumerate(p["near"])]]
+    p = order[r]
+    low, high = low_high(topo, cores, order, r)
+    if len(p["ids"]) > 1:
+        return [[(h, share(high, i, 2)) for i, (h, _) in enumerate(p["ids"])], [(cores[j], low[:4]) for j in p["near"]]]
+    return [[(p["ids"][0][0], low[:4])], [(cores[j], low[2 + 2 * i:4 + 2 * i]) for i, j in enumerate(p["near"])]]
 
 
 def ids_count(topo, cores, order, r, to):
     return [len(es) for call in ids_calls(topo, cores, order, r) for d, es in call if d == to][0]
 
 
-def near_engines(topo, cores, order, r, j):
-    es = engines(topo.mask(cores[r], cores[j]))
-    i = order[r]["near"].index(j)
-    if i == 0:
-        return es
-    n = len(es) // 2
-    return es[n * (i - 1):n * i]
-
-
-def relay_count(topo, core, relay):
-    return engines(topo.mask(core, relay))
+def tile_calls(topo, cores, order, r):
+    c, p = cores[r], order[r]
+    low, high = low_high(topo, cores, order, r)
+    first, rest = p["near"][0], p["near"][1:]
+    idle = p["relays"][len(p["ids"]):]
+    w = NC // len(idle)
+    out = [(CODES, [(first, cores[first], low, 0, NC)]),
+           (SCALES, [(first, h, share(high, i, len(idle)), w * i, w * i + w) for i, h in enumerate(idle)])]
+    if rest:
+        out += [(kind, [(j, cores[j], share(low, i, len(rest)), 0, NC) for i, j in enumerate(rest)]) for kind in (CODES, SCALES)]
+    for j in p["far"]:
+        for kind in (CODES, SCALES):
+            h = p["carry"][j][kind]
+            out.append((kind, [(j, h, engines(topo.mask(c, h)), 0, NC)]))
+    return out
 
 
 def dst(topo, to, frm):
@@ -126,23 +136,26 @@ def cut(buf, t, w=NC):
     return buf[:, w * t:w * t + w]
 
 
-def codes(buf, t):
-    return cut(buf, t).bitcast(dt.uint8)
+def piece(pair, kind, t, a, b):
+    v = pair[kind][:, NC * t + a:NC * t + b]
+    return v.bitcast(dt.uint8) if kind == CODES else v
 
 
-def relay_program(g, core, T, topo, r, far, order):
+def relay_program(g, core, T, topo, r, order):
     cores, S = T.cores, T.sem
-    es = engines(topo.mask(core, cores[far[0]]))
-    n = len(es) // len(far)
-    ar, m = S["ar%d" % r], len(relay_count(topo, cores[r], core))
-    g.wait_ge(S.rid, ids_count(topo, cores, order, r, core))
-    sent = send(g, T, topo, core, [(cores[j], T.xin[:, SL * r:SL * r + K], T.xrel[:, 0:K], S["id%d" % r], es[n * i:n * i + n])
-                                   for i, j in enumerate(far)])
-    for i, j in enumerate(far):
-        g.wait_ge(S["rc%d" % i], m)
-        sent += send(g, T, topo, core, [(cores[j], codes(T.lc, r), codes(T.rc, i), ar, es)])
-        g.wait_ge(S["rs%d" % i], m)
-        sent += send(g, T, topo, core, [(cores[j], cut(T.ls, r), cut(T.rs, i), ar, es)])
+    ar, sent = S["ar%d" % r], 0
+    for h, far in order[r]["ids"]:
+        if h == core:
+            es = engines(topo.mask(core, cores[far[0]]))
+            g.wait_ge(S.rid, ids_count(topo, cores, order, r, core))
+            sent += send(g, T, topo, core, [(cores[j], T.xin[:, SL * r:SL * r + K], T.xrel[:, 0:K], S["id%d" % r], share(es, i, len(far)))
+                                            for i, j in enumerate(far)])
+    for kind, parts in tile_calls(topo, cores, order, r):
+        for j, h, es, a, b in parts:
+            if h == core:
+                g.wait_ge(S[("rc%d", "rs%d")[kind] % j], len(es))
+                sent += send(g, T, topo, core, [(cores[j], piece((T.lc, T.ls), kind, r, a, b), piece((T.rc, T.rs), kind, j, a, b), ar,
+                                                 engines(topo.mask(core, cores[j])))])
     g.wait_ge(S.sent, sent)
 
 
@@ -154,14 +167,13 @@ def rank_program(g, core, T, topo):
     order = plan(cores, topo)
     if rank is None:
         for r in range(N):
-            for h, far in order[r]["relays"]:
-                if h == core:
-                    relay_program(g, core, T, topo, r, far, order)
+            if core in order[r]["relays"]:
+                relay_program(g, core, T, topo, r, order)
         return
     A, F = AluOpType, ActivationFunctionType
     S = T.sem
     v, ac, te, sy = g.vector, g.scalar, g.tensor, g.sync
-    near, far, relays = order[rank]["near"], order[rank]["far"], order[rank]["relays"]
+    near, far = order[rank]["near"], order[rank]["far"]
     work = [rank] + near + far
 
     sy.dma_start(T.idl[:, 0:K], T.tg[0:4, 0:NC]).then_inc(S.ldo, 16)
@@ -209,9 +221,9 @@ def rank_program(g, core, T, topo):
     def id_count(r):
         if rank in order[r]["near"]:
             return ids_count(topo, cores, order, r, core)
-        for h, fr in order[r]["relays"]:
+        for h, fr in order[r]["ids"]:
             if rank in fr:
-                return len(engines(topo.mask(h, core))) // len(fr)
+                return len(share(engines(topo.mask(h, core)), 0, len(fr)))
 
     def spread(ts):
         for t in ts:
@@ -283,31 +295,22 @@ def rank_program(g, core, T, topo):
             ac.wait_ge(S["z%d_%d" % (t, f)], 1)
             ac.activation(T.e[:, 4 * NC * t + f:4 * NC * (t + 1):4], T.z[:, bank:bank + NC], F.Copy).then_inc(S["ev%d" % t], 1)
 
-    groups = [[1]] + ([[2, 3]] if len(near) == 3 else []) + [[t] for t in range(1 + len(near), N)]
-    for ts in groups:
-        for t in ts:
-            g.wait_ge(S["qe%d" % t], 1)
-        pc, ps = [], []
-        for t in ts:
-            j = work[t]
-            if j in near:
-                es, ar = near_engines(topo, cores, order, rank, j), S["ar%d" % rank]
-                pc.append((cores[j], codes(T.lc, rank), codes(T.qe, t), ar, es))
-                ps.append((cores[j], cut(T.ls, rank), cut(T.se, t), ar, es))
+    for kind, parts in tile_calls(topo, cores, order, rank):
+        out = []
+        for j, d, es, a, b in parts:
+            t = work.index(j)
+            if kind == CODES:
+                g.wait_ge(S["qe%d" % t], 1)
+            src = piece((T.qe, T.se), kind, t, a, b)
+            if d == cores[j]:
+                out.append((d, piece((T.lc, T.ls), kind, rank, a, b), src, S["ar%d" % rank], es))
             else:
-                h, fr = [(h, fr) for h, fr in relays if j in fr][0]
-                i, es = fr.index(j), relay_count(topo, core, h)
-                pc.append((h, codes(T.rc, i), codes(T.qe, t), S["rc%d" % i], es))
-                ps.append((h, cut(T.rs, i), cut(T.se, t), S["rs%d" % i], es))
-        sent += send(g, T, topo, core, pc)
-        sent += send(g, T, topo, core, ps)
+                out.append((d, piece((T.rc, T.rs), kind, j, a, b), src, S[("rc%d", "rs%d")[kind] % j], es))
+        sent += send(g, T, topo, core, out)
 
     def tile_count(r):
-        if rank in order[r]["near"]:
-            return 2 * len(near_engines(topo, cores, order, r, rank))
-        for h, fr in order[r]["relays"]:
-            if rank in fr:
-                return 2 * len(engines(topo.mask(h, core)))
+        return sum(len(es) if d == core else len(engines(topo.mask(d, core)))
+                   for _, parts in tile_calls(topo, cores, order, r) for j, d, es, _, _ in parts if j == rank)
 
     te.wait_ge(S.qws, 1)
     te.wait_ge(S["ev4"], 4)

import math
from concourse.bass import DstId, RemoteDMATransfer
from concourse.mybir import AluOpType, ActivationFunctionType, dt

N = 6
NC = 192
G = 32
K = NC // G
SL = 8
SIM = 256
CODES, SCALES = 0, 1

SCRATCH = {
    "idl": ("sbuf", [128, 3 * SL], "bfloat16"),
    "idf": ("sbuf", [128, 3 * SL], "bfloat16"),
    "idu": ("sbuf", [128, SL], "bfloat16"),
    "x": ("sbuf", [128, SL], "bfloat16"),
    "xin": ("sbuf", [128, N * SL], "bfloat16"),
    "xrel": ("sbuf", [128, SL], "bfloat16"),
    "ip": ("sbuf", [128, 1], "float32"),
    "ij": ("sbuf", [128, 4], "float32"),
    "pw": ("sbuf", [128, 4], "bfloat16"),
    "key": ("sbuf", [128, 4], "bfloat16"),
    "hold": ("sbuf", [128, NC], "bfloat16"),
    "seed": ("sbuf", [128, N * NC], "bfloat16"),
    "spr": ("sbuf", [128, N * NC], "bfloat16"),
    "xt": ("sbuf", [128, N * NC], "bfloat16"),
    "o": ("sbuf", [128, N * 4 * NC], "bfloat16"),
    "qo": ("sbuf", [128, N * NC], "float8_e4m3fn_x4"),
    "so": ("sbuf", [128, N * NC], "uint8"),
    "tb": ("sbuf", [128, 4 * 512], "bfloat16"),
    "qt": ("sbuf", [128, 512], "float8_e4m3fn_x4"),
    "st": ("sbuf", [128, 512], "uint8"),
    "wb": ("sbuf", [128, 512], "bfloat16"),
    "qw": ("sbuf", [128, 128], "float8_e4m3fn_x4"),
    "sw": ("sbuf", [128, 128], "uint8"),
    "e": ("sbuf", [128, N * 4 * NC], "bfloat16"),
    "qe": ("sbuf", [128, N * NC], "float8_e4m3fn_x4"),
    "se": ("sbuf", [128, N * NC], "uint8"),
    "lc": ("sbuf", [128, N * NC], "float8_e4m3fn_x4"),
    "ls": ("sbuf", [128, N * NC], "uint8"),
    "rc": ("sbuf", [128, N * NC], "float8_e4m3fn_x4"),
    "rs": ("sbuf", [128, N * NC], "uint8"),
    "ysb": ("sbuf", [128, NC], "float32"),
    "z": ("psum", [128, 8 * 512], "float32"),
}
SEMAPHORES = (["ldo", "ldp", "ldb", "ldt0", "ldt1", "ldw", "iop", "ioj", "exk", "exo", "exb", "ms", "mh", "mz", "kk", "pa", "uu", "xx",
               "rid", "sent", "qws", "yy", "yv", "yst"]
              + ["qt%d" % f for f in range(4)]
              + [s + str(t) for s in ("id", "cp", "sc", "tr", "cm", "qo", "ev", "qe", "ar", "rc", "rs") for t in range(N)]
              + ["z%d_%d" % (t, f) for t in range(N) for f in range(4)])


def engines(mask):
    return [i for i in range(16) if mask >> i & 1]


def bits(es):
    return sum(1 << i for i in es)


def share(es, i, n):
    k = len(es) // n
    return es[k * i:k * i + k]


def plan(cores, topo):
    out = []
    seen = {}
    for c in cores:
        near = [j for j in range(N) if cores[j] != c and topo.may_write(c, cores[j])]
        far = [j for j in range(N) if cores[j] != c and j not in near]
        helpers = [h for h in range(SIM)
                   if h != c and topo.chip(h) == topo.chip(c) and topo.host(h) == topo.host(c)
                   and all(topo.may_write(h, cores[j]) for j in far)]
        same = [h for h in helpers if topo.die(h) == topo.die(c)]
        other = [h for h in helpers if topo.die(h) != topo.die(c)]
        relays = [h for two in zip(same, other) for h in two][:len(far)]
        k = seen.get(len(far), 0)
        seen[len(far)] = k + 1
        s = k * len(far) // 4 % 2
        flip = k % 2 if len(far) == 2 else 0
        far = far[s:] + far[:s]
        n = max(1, len(far) // 2)
        out.append({"near": near, "far": far, "relays": relays, "ids": [(h, far[i::n]) for i, h in enumerate(relays[:n])],
                    "carry": {j: (relays[i ^ flip], relays[i ^ flip ^ 1]) for i, j in enumerate(far)}})
    return out


def low_high(topo, cores, order, r):
    low = engines(topo.mask(cores[r], cores[order[r]["near"][0]]))
    return low, [e for e in engines(topo.mask(cores[r], order[r]["relays"][0])) if e not in low]


def ids_calls(topo, cores, order, r):
    p = order[r]
    low, high = low_high(topo, cores, order, r)
    if len(p["ids"]) > 1:
        return [[(h, share(high, i, 2)) for i, (h, _) in enumerate(p["ids"])], [(cores[j], low[:4]) for j in p["near"]]]
    return [[(p["ids"][0][0], low[:4])], [(cores[j], low[2 + 2 * i:4 + 2 * i]) for i, j in enumerate(p["near"])]]


def ids_count(topo, cores, order, r, to):
    return [len(es) for call in ids_calls(topo, cores, order, r) for d, es in call if d == to][0]


def tile_calls(topo, cores, order, r):
    c, p = cores[r], order[r]
    low, high = low_high(topo, cores, order, r)
    first, rest = p["near"][0], p["near"][1:]
    idle = p["relays"][len(p["ids"]):]
    w = NC // len(idle)
    out = [(CODES, [(first, cores[first], low, 0, NC)]),
           (SCALES, [(first, h, share(high, i, len(idle)), w * i, w * i + w) for i, h in enumerate(idle)])]
    if rest:
        out += [(kind, [(j, cores[j], share(low, i, len(rest)), 0, NC) for i, j in enumerate(rest)]) for kind in (CODES, SCALES)]
    for j in p["far"]:
        for kind in (CODES, SCALES):
            h = p["carry"][j][kind]
            out.append((kind, [(j, h, engines(topo.mask(c, h)), 0, NC)]))
    return out


def dst(topo, to, frm):
    rid, pnc = topo.addr(to, frm)
    return DstId(rid=rid, pnc=pnc)


def send(g, T, topo, core, parts):
    g.remote_dma_fused([RemoteDMATransfer(dst_ids=[dst(topo, to, core)], dma_engine_mask=bits(es), remote_sem=sem, src=in_, dst=out)
                        for to, out, in_, sem, es in parts], local_sem=T.sem.sent)
    return sum(len(p[4]) for p in parts)


def cut(buf, t, w=NC):
    return buf[:, w * t:w * t + w]


def piece(pair, kind, t, a, b):
    v = pair[kind][:, NC * t + a:NC * t + b]
    return v.bitcast(dt.uint8) if kind == CODES else v


def relay_program(g, core, T, topo, r, order):
    cores, S = T.cores, T.sem
    ar, sent = S["ar%d" % r], 0
    for h, far in order[r]["ids"]:
        if h == core:
            es = engines(topo.mask(core, cores[far[0]]))
            g.wait_ge(S.rid, ids_count(topo, cores, order, r, core))
            sent += send(g, T, topo, core, [(cores[j], T.xin[:, SL * r:SL * r + K], T.xrel[:, 0:K], S["id%d" % r], share(es, i, len(far)))
                                            for i, j in enumerate(far)])
    for kind, parts in tile_calls(topo, cores, order, r):
        for j, h, es, a, b in parts:
            if h == core:
                g.wait_ge(S[("rc%d", "rs%d")[kind] % j], len(es))
                sent += send(g, T, topo, core, [(cores[j], piece((T.lc, T.ls), kind, r, a, b), piece((T.rc, T.rs), kind, j, a, b), ar,
                                                 engines(topo.mask(core, cores[j])))])
    g.wait_ge(S.sent, sent)


def rank_program(g, core, T, topo):
    rank = T.rank_of(core)
    cores = T.cores
    if rank is None and not any(topo.chip(core) == topo.chip(c) and topo.host(core) == topo.host(c) for c in cores):
        return
    order = plan(cores, topo)
    if rank is None:
        for r in range(N):
            if core in order[r]["relays"]:
                relay_program(g, core, T, topo, r, order)
        return
    A, F = AluOpType, ActivationFunctionType
    S = T.sem
    v, ac, te, sy = g.vector, g.scalar, g.tensor, g.sync
    near, far = order[rank]["near"], order[rank]["far"]
    work = [rank] + near + far

    sy.dma_start(T.idl[:, 0:K], T.tg[0:4, 0:NC]).then_inc(S.ldo, 16)
    ac.dma_start(T.idl[:, 2 * SL:2 * SL + K], T.tg[0:4, 2 * NC:3 * NC]).then_inc(S.ldb, 16)
    sy.dma_start(T.idl[:, SL:SL + K], T.tg[0:4, NC:2 * NC]).then_inc(S.ldp, 16)
    sy.dma_start(T.tb[:, 0:1024], T.tab[:, 0:1024]).then_inc(S.ldt0, 16)
    sy.dma_start(T.tb[:, 1024:2048], T.tab[:, 1024:2048]).then_inc(S.ldt1, 16)
    sy.dma_start(T.wb[:], T.w[:]).then_inc(S.ldw, 16)

    g.iota(T.ij[:], [[1, 4]], 4 * rank, 0, allow_small_or_imprecise_dtypes=True).then_inc(S.ioj, 1)
    g.iota(T.ip[:], [[1, 1]], 128, 1, allow_small_or_imprecise_dtypes=True).then_inc(S.iop, 1)
    v.memset(T.hold[:], 1.0).then_inc(S.mh, 1)
    v.memset(T.seed[:], 0.0).then_inc(S.ms, 1)
    v.wait_ge(S.mh, 1)
    v.memset(T.hold[:, 0:NC:G], 0.0).then_inc(S.mz, 1)

    ln2 = math.log(2.0)
    ac.wait_ge(S.ioj, 1)
    ac.activation(T.pw[:], T.ij[:], F.Exp, scale=ln2).then_inc(S.exk, 1)
    ac.wait_ge(S.ldo, 16)
    ac.activation(T.idf[:, 0:K], T.idl[:, 0:K], F.Exp, scale=4 * ln2).then_inc(S.exo, 1)
    ac.wait_ge(S.ldb, 16)
    ac.activation(T.idf[:, 2 * SL:2 * SL + K], T.idl[:, 2 * SL:2 * SL + K], F.Exp, scale=ln2).then_inc(S.exb, 1)

    v.wait_ge(S.ldp, 16)
    v.tensor_scalar(T.idf[:, SL:SL + K], T.idl[:, SL:SL + K], 128.0, None, A.add).then_inc(S.pa, 1)
    v.wait_ge(S.pa, 1)
    v.wait_ge(S.exo, 1)
    v.tensor_tensor(T.idu[:, 0:K], T.idf[:, SL:SL + K], T.idf[:, 0:K], A.mult).then_inc(S.uu, 1)
    v.wait_ge(S.uu, 1)
    v.wait_ge(S.exb, 1)
    v.tensor_tensor(T.x[:, 0:K], T.idu[:, 0:K], T.idf[:, 2 * SL:2 * SL + K], A.mult).then_inc(S.xx, 1)

    sent = 0
    g.wait_ge(S.xx, 1)
    for call in ids_calls(topo, cores, order, rank):
        parts = []
        for d, es in call:
            if T.rank_of(d) is None:
                parts.append((d, T.xrel[:, 0:K], T.x[:, 0:K], S.rid, es))
            else:
                parts.append((d, T.xin[:, SL * rank:SL * rank + K], T.x[:, 0:K], S["id%d" % rank], es))
        sent += send(g, T, topo, core, parts)

    def id_count(r):
        if rank in order[r]["near"]:
            return ids_count(topo, cores, order, r, core)
        for h, fr in order[r]["ids"]:
            if rank in fr:
                return len(share(engines(topo.mask(h, core)), 0, len(fr)))

    def spread(ts):
        for t in ts:
            j = work[t]
            if j == rank:
                v.wait_ge(S.xx, 1)
                src = T.x[:, 0:K]
            else:
                v.wait_ge(S["id%d" % j], id_count(j))
                src = T.xin[:, SL * j:SL * j + K]
            v.tensor_copy(T.seed[:, NC * t:NC * t + NC:G], src).then_inc(S["cp%d" % t], 1)
        for t in ts:
            v.wait_ge(S["cp%d" % t], 1)
            v.tensor_tensor_scan(cut(T.spr, t), T.hold[:], cut(T.seed, t), 0.0, A.mult, A.add).then_inc(S["sc%d" % t], 1)
        for t in ts:
            v.wait_ge(S["sc%d" % t], 1)
            v.transpose(cut(T.xt, t), cut(T.spr, t)).then_inc(S["tr%d" % t], 1)

    def match(t):
        v.wait_ge(S["tr%d" % t], 1)
        for b in range(4):
            v.tensor_scalar(T.o[:, 4 * NC * t + b:4 * NC * (t + 1):4], cut(T.xt, t), T.key[:, b:b + 1], None,
                            A.is_equal).then_inc(S["cm%d" % t], 1)
        v.wait_ge(S["cm%d" % t], 4)
        v.quantize_mx(cut(T.qo, t), cut(T.so, t), cut(T.o, t, 4 * NC)).then_inc(S["qo%d" % t], 1)

    def pack(t):
        v.wait_ge(S["ev%d" % t], 4)
        v.quantize_mx(cut(T.qe, t), cut(T.se, t), cut(T.e, t, 4 * NC)).then_inc(S["qe%d" % t], 1)

    v.wait_ge(S.ms, 1)
    v.wait_ge(S.mz, 1)
    spread([0])
    v.wait_ge(S.exk, 1)
    v.wait_ge(S.iop, 1)
    v.tensor_scalar(T.key[:], T.pw[:], T.ip[:, 0:1], None, A.mult).then_inc(S.kk, 1)
    v.wait_ge(S.kk, 1)
    match(0)
    for f in range(4):
        if f % 2 == 0:
            v.wait_ge(S["ldt%d" % (f // 2)], 16)
        v.quantize_mx(cut(T.qt, f, 128), cut(T.st, f, 128), cut(T.tb, f, 512)).then_inc(S["qt%d" % f], 1)
    v.wait_ge(S.ldw, 16)
    v.quantize_mx(T.qw[:], T.sw[:], T.wb[:]).then_inc(S.qws, 1)
    pack(0)
    if len(near) == 3:
        steps = [(spread, [1, 2]), (match, 1), (match, 2), (spread, [3]), (pack, 1), (match, 3), (pack, 2), (pack, 3),
                 (spread, [4, 5]), (match, 4), (match, 5), (pack, 4), (pack, 5)]
    else:
        steps = [(spread, [1]), (match, 1), (pack, 1), (spread, [2, 3]), (match, 2), (match, 3), (spread, [4, 5]),
                 (pack, 2), (match, 4), (pack, 3), (match, 5), (pack, 4), (pack, 5)]
    for step, t in steps:
        step(t)

    for t in range(N):
        te.wait_ge(S["qo%d" % t], 1)
        if t >= 2:
            te.wait_ge(S["ev%d" % (t - 2)], 4)
        for f in range(4):
            if t == 0:
                te.wait_ge(S["qt%d" % f], 1)
            bank = 512 * (4 * (t % 2) + f)
            te.matmul_mx(T.z[:, bank:bank + NC], cut(T.qt, f, 128), cut(T.st, f, 128), cut(T.qo, t), cut(T.so, t), True, True
                         ).then_inc(S["z%d_%d" % (t, f)], 1)

    for t in range(N):
        for f in range(4):
            bank = 512 * (4 * (t % 2) + f)
            ac.wait_ge(S["z%d_%d" % (t, f)], 1)
            ac.activation(T.e[:, 4 * NC * t + f:4 * NC * (t + 1):4], T.z[:, bank:bank + NC], F.Copy).then_inc(S["ev%d" % t], 1)

    for kind, parts in tile_calls(topo, cores, order, rank):
        out = []
        for j, d, es, a, b in parts:
            t = work.index(j)
            if kind == CODES:
                g.wait_ge(S["qe%d" % t], 1)
            src = piece((T.qe, T.se), kind, t, a, b)
            if d == cores[j]:
                out.append((d, piece((T.lc, T.ls), kind, rank, a, b), src, S["ar%d" % rank], es))
            else:
                out.append((d, piece((T.rc, T.rs), kind, j, a, b), src, S[("rc%d", "rs%d")[kind] % j], es))
        sent += send(g, T, topo, core, out)

    def tile_count(r):
        return sum(len(es) if d == core else len(engines(topo.mask(d, core)))
                   for _, parts in tile_calls(topo, cores, order, r) for j, d, es, _, _ in parts if j == rank)

    te.wait_ge(S.qws, 1)
    te.wait_ge(S["ev4"], 4)
    for t in range(N):
        j = work[t]
        if t == 0:
            te.wait_ge(S.qe0, 1)
            c, s = cut(T.qe, 0), cut(T.se, 0)
        else:
            te.wait_ge(S["ar%d" % j], tile_count(j))
            c, s = cut(T.lc, j), cut(T.ls, j)
        mm = te.matmul_mx(T.z[:, 0:NC], T.qw[:], T.sw[:], c, s, t == 0, t == N - 1)
    mm.then_inc(S.yy, 1)
    v.wait_ge(S.yy, 1)
    for k in range(K):
        v.tensor_copy(T.ysb[:, k:NC:K], T.z[:, G * k:G * k + G]).then_inc(S.yv, 1)
    sy.wait_ge(S.yv, K)
    sy.dma_start(T.y[:], T.ysb[:]).then_inc(S.yst, 16)
    sy.wait_ge(S.yst, 16)
    g.wait_ge(S.sent, sent)
